import numpy as np
import ml_dtypes


def mxq(x, axis, fmt="e4m3"):
    dtype, down = {"e4m3": (ml_dtypes.float8_e4m3fn, 7), "e5m2": (ml_dtypes.float8_e5m2, 14)}[fmt]
    v = np.moveaxis(np.asarray(x, np.float32).astype(ml_dtypes.bfloat16).astype(np.float64), axis, -1)
    blocks = v.reshape(v.shape[:-1] + (-1, 32))
    amax = np.abs(blocks).max(-1, keepdims=True)
    byte = np.maximum(np.where(amax > 0, np.frexp(amax)[1] - 1 + 127, 0) - down, 1)
    scale = np.exp2(byte - 127.0)
    codes = (blocks / scale).astype(np.float32).astype(dtype).astype(np.float64)
    return np.moveaxis((codes * scale).reshape(v.shape), -1, axis)


WIDE = False


def mx_kscale(k):
    if not WIDE:
        return np.ones(k)
    levels = np.array([10, -10, 5, -5, 0])
    if k % 512:
        return np.exp2(np.random.permutation(np.resize(levels, k // 32))).repeat(32)
    a = np.empty((k // 512, 16))
    for p in range(k // 512):
        a[p, :8] = np.random.permutation(np.resize(levels, 8))
        for g in range(8):
            far = levels[np.abs(levels - a[p, g]) >= 10]
            a[p, g + 8] = far[np.random.randint(len(far))]
    return np.exp2(a.ravel()).repeat(32)


def f64(x):
    return np.asarray(x).astype(np.float64)


def striped(idx):
    return np.tile(np.asarray(idx).reshape(-1, 16).T, (8, 1)).astype(np.uint16)


def unstriped(offs):
    return offs[:16].T.reshape(-1).astype(np.int64)


E2M1 = np.array([0.0, 0.5, 1.0, 1.5, 2.0, 3.0, 4.0, 6.0, -0.0, -0.5, -1.0, -1.5, -2.0, -3.0, -4.0, -6.0])


def pack_weight(w, fmt):
    k, n = w.shape
    w = f64(np.asarray(w, np.float32).astype(ml_dtypes.bfloat16)).reshape(k // 32, 32, n)
    amax = np.abs(w).max(1)
    if fmt == "e4m3":
        byte = np.frexp(amax)[1] - 1 + 127 - 7
    else:
        mant, ex = np.frexp(amax / 6.0)
        byte = np.where(mant > 0.5, ex, ex - 1) + 127
    byte = np.clip(np.where(amax > 0, byte, 1), 1, 254)
    scaled = (w * np.exp2(127.0 - byte)[:, None, :]).reshape(k, n).astype(np.float32)
    by_word = np.ascontiguousarray(scaled.reshape(k // 512, 128, 4, n).transpose(0, 1, 3, 2))
    if fmt == "e4m3":
        words = by_word.astype(ml_dtypes.float8_e4m3fn).view(np.uint8)
    else:
        c = by_word.astype(ml_dtypes.float4_e2m1fn).view(np.uint8) & 0xF
        words = (c[..., 0::2] | (c[..., 1::2] << 4)).reshape(k // 512, 128, 2 * n)
    return np.ascontiguousarray(words), np.ascontiguousarray(byte.astype(np.uint8).reshape(k // 512, 16, n))


def unpack_weight(words, scales, fmt):
    g, _, n = scales.shape
    words = np.ascontiguousarray(words).reshape(g, 128, n, -1)
    if fmt == "e4m3":
        vals = words.view(ml_dtypes.float8_e4m3fn).astype(np.float64)
    else:
        nib = np.empty((g, 128, n, 4), np.uint8)
        nib[..., 0::2] = words & 0xF
        nib[..., 1::2] = words >> 4
        vals = E2M1[nib]
    vals = vals * np.repeat(np.exp2(scales.astype(np.float64) - 127.0), 8, axis=1)[..., None]
    return vals.transpose(0, 1, 3, 2).reshape(g * 512, n)


D, K, T, M, I, E = 512, 512, 2048, 1024, 512, 256


def setup_inputs():
    n = np.random.standard_normal
    idx = np.random.permutation(T)[:I]
    idx2 = np.random.permutation(M)[:I]
    idx3 = np.random.permutation(M)[:I]
    fd = mx_kscale(D)
    fk = mx_kscale(K)
    pagesp = pack_weight(n((D, T)) / fd[:, None], "e4m3")
    wap = pack_weight(n((D, K)) * 1.0 / np.sqrt(D) * fd[:, None], "e2m1")
    wop = pack_weight(n((K, E)) * 1.0 / np.sqrt(K) / fk[:, None], "e2m1")
    return {
        "pages_words": pagesp[0],
        "pages_scales": pagesp[1],
        "wa_words": wap[0],
        "wa_scales": wap[1],
        "kf": (np.random.uniform(0.5, 2.0, (K, 1)) * fk[:, None]).astype(np.float32),
        "wo_words": wop[0],
        "wo_scales": wop[1],
        "offs": striped(idx),
        "offs2": striped(idx2),
        "offs3": striped(idx3),
    }


def reference(pages_words, pages_scales, wa_words, wa_scales, kf, wo_words, wo_scales, offs, offs2, offs3):
    idx = unstriped(offs)
    idx2 = unstriped(offs2)
    idx3 = unstriped(offs3)
    pagesu = unpack_weight(pages_words, pages_scales, "e4m3")
    wau = unpack_weight(wa_words, wa_scales, "e2m1")
    wou = unpack_weight(wo_words, wo_scales, "e2m1")
    pagesidxg = pagesu[:, idx]
    z = wau.T @ pagesidxg
    f1 = np.zeros((K, M))
    f1[:, idx2] = z
    v = f1[:, idx3] - z
    w = v * f64(kf)
    wq = mxq(w, 0, "e4m3")
    y = wou.T @ wq
    return y

@@ -1,0 +1,157 @@
+from contextlib import ExitStack
+
+import concourse.mybir as mybir
+
+D, K, T, M, I, E = 512, 512, 2048, 1024, 512, 256
+FLOPS = 2 * D * K * I + 2 * K * E * I
+
+F32 = mybir.dt.float32
+BF16 = mybir.dt.bfloat16
+I32 = mybir.dt.int32
+U32 = mybir.dt.uint32
+U16 = mybir.dt.uint16
+U8 = mybir.dt.uint8
+FP8X4 = mybir.dt.float8_e4m3fn_x4
+FP4X4 = mybir.dt.float4_e2m1fn_x4
+COPY = mybir.ActivationFunctionType.Copy
+MULT = mybir.AluOpType.mult
+SUB = mybir.AluOpType.subtract
+
+P = 128
+PACK = 4
+H = I // 2
+HC = H // 16
+
+
+def tile_attend_pagerelay_kernel(tc, pages_words, pages_scales, wa_words, wa_scales, kf, wo_words, wo_scales,
+                                  offs, offs2, offs3, out):
+    nc = tc.nc
+    with ExitStack() as ctx:
+        lists = ctx.enter_context(tc.tile_pool(name="lists", bufs=1))
+        sb = ctx.enter_context(tc.tile_pool(name="sb", bufs=1))
+        psum = ctx.enter_context(tc.psum_pool(name="psum", bufs=1))
+
+        def load_scale_rows(queue, plane, rows, q):
+            queue.dma_start(plane[32 * q:32 * q + 4, :].bitcast(I32), rows[0, 4 * q:4 * q + 4, :].bitcast(I32))
+
+        def half(h):
+            return slice(h * H, (h + 1) * H)
+
+        def cols(h):
+            return slice(h * HC, (h + 1) * HC)
+
+        idx = lists.tile([P, I // 16], U16, name="idx")
+        idx2 = lists.tile([P, I // 16], U16, name="idx2")
+        idx3 = lists.tile([P, I // 16], U16, name="idx3")
+        pool_words = sb.tile([P, T], U32, name="pool_words", align_bytes=64)
+        pool_scales = sb.tile([P, T], U8, name="pool_scales", align_bytes=64)
+        wa_raw = sb.tile([P, 2 * K], U8, name="wa_raw", align_bytes=64)
+        wa_scales_raw = sb.tile([P, K], U8, name="wa_scales_raw", align_bytes=64)
+        wo_codes = sb.tile([P, 2 * E], U8, name="wo_codes", align_bytes=64)
+        wo_plane = sb.tile([P, E], U8, name="wo_plane", align_bytes=64)
+        factor = sb.tile([P, PACK], F32, name="factor")
+
+        nc.vector.memset(pool_scales[:].bitcast(I32), 0)
+        nc.vector.memset(wa_scales_raw[:].bitcast(I32), 0)
+
+        nc.sync.dma_start(idx[:], offs)
+        nc.sync.dma_start(idx2[:], offs2)
+        nc.sync.dma_start(idx3[:], offs3)
+        nc.sync.dma_start(pool_words[:].bitcast(I32), pages_words[0].rearrange("p n t -> p (n t)").bitcast(I32))
+        for q in range(4):
+            load_scale_rows(nc.scalar, pool_scales, pages_scales, q)
+        for q in range(3):
+            load_scale_rows(nc.scalar, wa_scales_raw, wa_scales, q)
+        nc.gpsimd.dma_start(wa_raw[:].bitcast(I32), wa_words[0].bitcast(I32))
+        load_scale_rows(nc.gpsimd, wa_scales_raw, wa_scales, 3)
+        nc.gpsimd.dma_start(factor[:], kf.rearrange("(p t) o -> p (t o)", t=PACK))
+        nc.gpsimd.dma_start(wo_codes[:].bitcast(I32), wo_words[0].bitcast(I32))
+        nc.gpsimd.memset(wo_plane[:].bitcast(I32), 0)
+        for q in range(4):
+            load_scale_rows(nc.gpsimd, wo_plane, wo_scales, q)
+
+        f1 = [sb.tile([P, M], F32, name="f1_%d" % t) for t in range(PACK)]
+        for t in range(PACK):
+            nc.vector.memset(f1[t][:].bitcast(I32), 0)
+
+        page_scales = sb.tile([P, I], U8, name="page_scales", align_bytes=64)
+        nc.vector.tensor_copy(page_scales[:], pool_scales[:].indirect(idx[:]))
+
+        wa_codes = sb.tile([P, 2 * K], U8, name="wa_codes", align_bytes=64)
+        wa_plane = sb.tile([P, K], U8, name="wa_plane", align_bytes=64)
+        nc.vector.tensor_copy(wa_codes[:].bitcast(U16).rearrange("p (t m) -> p t m", t=PACK),
+                              wa_raw[:].bitcast(U16).rearrange("p (m t) -> p t m", t=PACK))
+        nc.vector.tensor_copy(wa_plane[:].rearrange("p (t m) -> p t m", t=PACK),
+                              wa_scales_raw[:].rearrange("p (m t) -> p t m", t=PACK))
+
+        page_words = sb.tile([P, I], U32, name="page_words", align_bytes=64)
+        for h in range(2):
+            nc.vector.tensor_copy(page_words[:, half(h)], pool_words[:].indirect(idx[:, cols(h)]))
+
+        def hidden(t, slots, bank):
+            nc.tensor.matmul_mx(out=bank, lhsT=wa_codes[:, 2 * P * t:2 * P * (t + 1)].bitcast(FP4X4),
+                                lhsT_scale=wa_plane[:, P * t:P * (t + 1)],
+                                rhs=page_words[:, slots].bitcast(FP8X4), rhs_scale=page_scales[:, slots],
+                                start=True, stop=True)
+
+        z = [sb.tile([P, I], F32, name="z_%d" % t) for t in range(PACK)]
+        zh = {}
+        for h in range(2):
+            for t in range(2):
+                zh[t, h] = psum.tile([P, H], F32, name="zh_%d_%d" % (t, h))
+                hidden(t, half(h), zh[t, h][:])
+        zb = {}
+        for t in range(2, 4):
+            zb[t] = psum.tile([P, I], F32, name="zb_%d" % t)
+            hidden(t, slice(0, I), zb[t][:])
+
+        for h in range(2):
+            nc.vector.tensor_copy(z[0][:, half(h)], zh[0, h][:])
+            nc.vector.tensor_copy(f1[0][:].indirect(idx2[:, cols(h)]), z[0][:, half(h)])
+            nc.scalar.copy(z[1][:, half(h)], zh[1, h][:])
+            nc.scalar.activation(f1[1][:].indirect(idx2[:, cols(h)]), z[1][:, half(h)], COPY)
+        for t in range(2, 4):
+            nc.scalar.copy(z[t][:], zb[t][:])
+            for h in range(2):
+                nc.scalar.activation(f1[t][:].indirect(idx2[:, cols(h)]), z[t][:, half(h)], COPY)
+
+        w = [sb.tile([P, H, PACK], BF16, name="w_%d" % h, align_bytes=64) for h in range(2)]
+
+        def weigh(t, h, v):
+            nc.vector.tensor_scalar(w[h][:, :, t], v[:, half(h)], factor[:, t:t + 1], None, MULT)
+
+        for t in range(3):
+            v = sb.tile([P, I], F32, name="v_%d" % (t % 2))
+            nc.vector.tensor_tensor(v[:], f1[t][:].indirect(idx3[:]), z[t][:], SUB)
+            for h in range(2):
+                weigh(t, h, v)
+
+        v = sb.tile([P, I], F32, name="v_0")
+        looked = sb.tile([P, H], F32, name="looked")
+        nc.scalar.activation(looked[:], f1[3][:].indirect(idx3[:, cols(1)]), COPY)
+        out_rows = out.rearrange("(j p) i -> p j i", p=P)
+        for h in range(2):
+            if h == 0:
+                nc.vector.tensor_tensor(v[:, half(h)], f1[3][:].indirect(idx3[:, cols(h)]), z[3][:, half(h)], SUB)
+            else:
+                nc.vector.tensor_tensor(v[:, half(h)], looked[:], z[3][:, half(h)], SUB)
+            weigh(3, h, v)
+            codes = sb.tile([P, H], U32, name="codes_%d" % h, align_bytes=64)
+            plane = sb.tile([P, H], U8, name="plane_%d" % h, align_bytes=64)
+            nc.vector.quantize_mx(out=codes[:].bitcast(FP8X4), scales=plane[:],
+                                  in_=w[h][:].rearrange("p i t -> p (i t)"))
+            for j in range(2):
+                y = psum.tile([P, H], F32, name="zh_%d_%d" % (j, h))
+                nc.tensor.matmul_mx(out=y[:], lhsT=wo_codes[:, 2 * P * j:2 * P * (j + 1)].bitcast(FP4X4),
+                                    lhsT_scale=wo_plane[:, P * j:P * (j + 1)],
+                                    rhs=codes[:].bitcast(FP8X4), rhs_scale=plane[:], start=True, stop=True)
+                res = sb.tile([P, H], F32, name="res_%d_%d" % (h, j))
+                if h == 1 and j == 0:
+                    nc.vector.tensor_copy(res[:], y[:])
+                    nc.sync.dma_start(out_rows[:, j, half(h)], res[:])
+                elif h == 1:
+                    nc.scalar.copy(res[:], y[:])
+                    nc.scalar.dma_start(out_rows[:, j, half(h)], res[:])
+                else:
+                    nc.scalar.copy(res[:], y[:])
+                    nc.sync.dma_start(out_rows[:, j, half(h)], res[:])

@@ -21,6 +21,7 @@ P = 128
 PACK = 4
 H = I // 2
 HC = H // 16
+SHARE = 128
 
 
 def tile_attend_pagerelay_kernel(tc, pages_words, pages_scales, wa_words, wa_scales, kf, wo_words, wo_scales,
@@ -47,46 +48,50 @@ def tile_attend_pagerelay_kernel(tc, pages_words, pages_scales, wa_words, wa_sca
         pool_scales = sb.tile([P, T], U8, name="pool_scales", align_bytes=64)
         wa_raw = sb.tile([P, 2 * K], U8, name="wa_raw", align_bytes=64)
         wa_scales_raw = sb.tile([P, K], U8, name="wa_scales_raw", align_bytes=64)
-        wo_codes = sb.tile([P, 2 * E], U8, name="wo_codes", align_bytes=64)
         wo_plane = sb.tile([P, E], U8, name="wo_plane", align_bytes=64)
-        factor = sb.tile([P, PACK], F32, name="factor")
 
         nc.vector.memset(pool_scales[:].bitcast(I32), 0)
         nc.vector.memset(wa_scales_raw[:].bitcast(I32), 0)
 
+        staged = sb.tile([P, T], U8, name="staged", align_bytes=64)
         nc.sync.dma_start(idx[:], offs)
+        for q in range(4):
+            load_scale_rows(nc.sync if q < 2 else nc.scalar, staged, pages_scales, q)
+        nc.scalar.dma_start(wa_raw[:].bitcast(I32), wa_words[0].bitcast(I32))
+        nc.sync.dma_start(pool_words[:].bitcast(I32), pages_words[0].rearrange("p n t -> p (n t)").bitcast(I32))
         nc.sync.dma_start(idx2[:], offs2)
         nc.sync.dma_start(idx3[:], offs3)
-        nc.sync.dma_start(pool_words[:].bitcast(I32), pages_words[0].rearrange("p n t -> p (n t)").bitcast(I32))
         for q in range(4):
-            load_scale_rows(nc.scalar, pool_scales, pages_scales, q)
-        for q in range(3):
             load_scale_rows(nc.scalar, wa_scales_raw, wa_scales, q)
-        nc.gpsimd.dma_start(wa_raw[:].bitcast(I32), wa_words[0].bitcast(I32))
-        load_scale_rows(nc.gpsimd, wa_scales_raw, wa_scales, 3)
-        nc.gpsimd.dma_start(factor[:], kf.rearrange("(p t) o -> p (t o)", t=PACK))
-        nc.gpsimd.dma_start(wo_codes[:].bitcast(I32), wo_words[0].bitcast(I32))
-        nc.gpsimd.memset(wo_plane[:].bitcast(I32), 0)
-        for q in range(4):
-            load_scale_rows(nc.gpsimd, wo_plane, wo_scales, q)
-
         f1 = [sb.tile([P, M], F32, name="f1_%d" % t) for t in range(PACK)]
         for t in range(PACK):
-            nc.vector.memset(f1[t][:].bitcast(I32), 0)
+            (nc.vector if t % 2 else nc.gpsimd).memset(f1[t][:].bitcast(I32), 0)
+        nc.gpsimd.memset(wo_plane[:].bitcast(I32), 0)
+
+        for q in range(4):
+            nc.vector.tensor_copy(pool_scales[32 * q:32 * q + 4, :].bitcast(I32), staged[32 * q:32 * q + 4, :].bitcast(I32))
 
         page_scales = sb.tile([P, I], U8, name="page_scales", align_bytes=64)
-        nc.vector.tensor_copy(page_scales[:], pool_scales[:].indirect(idx[:]))
 
         wa_codes = sb.tile([P, 2 * K], U8, name="wa_codes", align_bytes=64)
         wa_plane = sb.tile([P, K], U8, name="wa_plane", align_bytes=64)
-        nc.vector.tensor_copy(wa_codes[:].bitcast(U16).rearrange("p (t m) -> p t m", t=PACK),
-                              wa_raw[:].bitcast(U16).rearrange("p (m t) -> p t m", t=PACK))
-        nc.vector.tensor_copy(wa_plane[:].rearrange("p (t m) -> p t m", t=PACK),
-                              wa_scales_raw[:].rearrange("p (m t) -> p t m", t=PACK))
+        nc.scalar.copy(wa_codes[:].bitcast(U16).rearrange("p (t m) -> p t m", t=PACK),
+                       wa_raw[:].bitcast(U16).rearrange("p (m t) -> p t m", t=PACK))
 
         page_words = sb.tile([P, I], U32, name="page_words", align_bytes=64)
         for h in range(2):
+            nc.vector.tensor_copy(page_scales[:, half(h)], pool_scales[:].indirect(idx[:, cols(h)]))
             nc.vector.tensor_copy(page_words[:, half(h)], pool_words[:].indirect(idx[:, cols(h)]))
+            planes = slice(0, 1) if h == 0 else slice(1, PACK)
+            nc.vector.tensor_copy(wa_plane[:].rearrange("p (t m) -> p t m", t=PACK)[:, planes, :],
+                                  wa_scales_raw[:].rearrange("p (m t) -> p t m", t=PACK)[:, planes, :])
+
+        factor = sb.tile([P, PACK], F32, name="factor", tag="wa_raw", align_bytes=64)
+        nc.sync.dma_start(factor[:], kf.rearrange("(p t) o -> p (t o)", t=PACK))
+        wo_codes = sb.tile([P, 2 * E], U8, name="wo_codes", tag="staged", align_bytes=64)
+        nc.sync.dma_start(wo_codes[:].bitcast(I32), wo_words[0].bitcast(I32))
+        for q in range(4):
+            load_scale_rows(nc.sync, wo_plane, wo_scales, q)
 
         def hidden(t, slots, bank):
             nc.tensor.matmul_mx(out=bank, lhsT=wa_codes[:, 2 * P * t:2 * P * (t + 1)].bitcast(FP4X4),
@@ -95,53 +100,62 @@ def tile_attend_pagerelay_kernel(tc, pages_words, pages_scales, wa_words, wa_sca
                                 start=True, stop=True)
 
         z = [sb.tile([P, I], F32, name="z_%d" % t) for t in range(PACK)]
-        zh = {}
+        every = slice(0, I)
+        z0_banks = [psum.tile([P, H], F32, name="bank_%d" % h) for h in range(2)]
         for h in range(2):
-            for t in range(2):
-                zh[t, h] = psum.tile([P, H], F32, name="zh_%d_%d" % (t, h))
-                hidden(t, half(h), zh[t, h][:])
-        zb = {}
-        for t in range(2, 4):
-            zb[t] = psum.tile([P, I], F32, name="zb_%d" % t)
-            hidden(t, slice(0, I), zb[t][:])
+            hidden(0, half(h), z0_banks[h][:])
+        z1_bank = psum.tile([P, I], F32, name="bank_2")
+        hidden(1, every, z1_bank[:])
+        z3_first = psum.tile([P, SHARE], F32, name="bank_3")
+        hidden(3, slice(0, SHARE), z3_first[:])
+        z2_bank = psum.tile([P, I], F32, name="bank_4")
+        hidden(2, every, z2_bank[:])
+        z3_rest = psum.tile([P, I - SHARE], F32, name="bank_5")
+        hidden(3, slice(SHARE, H), z3_rest[:, :H - SHARE])
+        hidden(3, half(1), z3_rest[:, H - SHARE:])
 
-        for h in range(2):
-            nc.vector.tensor_copy(z[0][:, half(h)], zh[0, h][:])
-            nc.vector.tensor_copy(f1[0][:].indirect(idx2[:, cols(h)]), z[0][:, half(h)])
-            nc.scalar.copy(z[1][:, half(h)], zh[1, h][:])
-            nc.scalar.activation(f1[1][:].indirect(idx2[:, cols(h)]), z[1][:, half(h)], COPY)
-        for t in range(2, 4):
-            nc.scalar.copy(z[t][:], zb[t][:])
-            for h in range(2):
-                nc.scalar.activation(f1[t][:].indirect(idx2[:, cols(h)]), z[t][:, half(h)], COPY)
+        def put_scalar(t, slots):
+            nc.scalar.activation(f1[t][:].indirect(idx2[:, slots.start // 16:slots.stop // 16]), z[t][:, slots], COPY)
 
-        w = [sb.tile([P, H, PACK], BF16, name="w_%d" % h, align_bytes=64) for h in range(2)]
+        nc.vector.tensor_copy(z[1][:], z1_bank[:])
+        nc.vector.tensor_copy(z[3][:, :SHARE], z3_first[:])
+        nc.vector.tensor_copy(f1[1][:].indirect(idx2[:]), z[1][:])
+        nc.vector.tensor_copy(f1[3][:].indirect(idx2[:, :SHARE // 16]), z[3][:, :SHARE])
 
-        def weigh(t, h, v):
-            nc.vector.tensor_scalar(w[h][:, :, t], v[:, half(h)], factor[:, t:t + 1], None, MULT)
+        nc.scalar.copy(z[0][:, half(0)], z0_banks[0][:])
+        put_scalar(0, half(0))
+        nc.scalar.copy(z[0][:, half(1)], z0_banks[1][:])
+        nc.scalar.copy(z[2][:], z2_bank[:])
+        put_scalar(2, half(0))
+        nc.scalar.copy(z[3][:, SHARE:], z3_rest[:])
+        put_scalar(0, half(1))
+        put_scalar(2, half(1))
+        put_scalar(3, slice(SHARE, I))
 
-        for t in range(3):
-            v = sb.tile([P, I], F32, name="v_%d" % (t % 2))
+        w = sb.tile([P, I, PACK], BF16, name="w", align_bytes=64)
+
+        def weigh(t, slots, v):
+            nc.vector.tensor_scalar(w[:, slots, t], v[:, slots], factor[:, t:t + 1], None, MULT)
+
+        for n, t in enumerate((1, 0, 2)):
+            v = sb.tile([P, I], F32, name="v_%d" % (n % 2))
             nc.vector.tensor_tensor(v[:], f1[t][:].indirect(idx3[:]), z[t][:], SUB)
-            for h in range(2):
-                weigh(t, h, v)
+            weigh(t, every, v)
 
         v = sb.tile([P, I], F32, name="v_0")
-        looked = sb.tile([P, H], F32, name="looked")
-        nc.scalar.activation(looked[:], f1[3][:].indirect(idx3[:, cols(1)]), COPY)
+        looked = sb.tile([P, I], F32, name="looked")
+        for h in range(2):
+            nc.scalar.activation(looked[:, half(h)], f1[3][:].indirect(idx3[:, cols(h)]), COPY)
         out_rows = out.rearrange("(j p) i -> p j i", p=P)
         for h in range(2):
-            if h == 0:
-                nc.vector.tensor_tensor(v[:, half(h)], f1[3][:].indirect(idx3[:, cols(h)]), z[3][:, half(h)], SUB)
-            else:
-                nc.vector.tensor_tensor(v[:, half(h)], looked[:], z[3][:, half(h)], SUB)
-            weigh(3, h, v)
+            nc.vector.tensor_tensor(v[:, half(h)], looked[:, half(h)], z[3][:, half(h)], SUB)
+            weigh(3, half(h), v)
             codes = sb.tile([P, H], U32, name="codes_%d" % h, align_bytes=64)
             plane = sb.tile([P, H], U8, name="plane_%d" % h, align_bytes=64)
             nc.vector.quantize_mx(out=codes[:].bitcast(FP8X4), scales=plane[:],
-                                  in_=w[h][:].rearrange("p i t -> p (i t)"))
+                                  in_=w[:, half(h), :].rearrange("p i t -> p (i t)"))
             for j in range(2):
-                y = psum.tile([P, H], F32, name="zh_%d_%d" % (j, h))
+                y = psum.tile([P, H], F32, name="bank_%d" % (2 * h + j))
                 nc.tensor.matmul_mx(out=y[:], lhsT=wo_codes[:, 2 * P * j:2 * P * (j + 1)].bitcast(FP4X4),
                                     lhsT_scale=wo_plane[:, P * j:P * (j + 1)],
                                     rhs=codes[:].bitcast(FP8X4), rhs_scale=plane[:], start=True, stop=True)

@@ -78,13 +78,12 @@ def tile_attend_pagerelay_kernel(tc, pages_words, pages_scales, wa_words, wa_sca
         nc.scalar.copy(wa_codes[:].bitcast(U16).rearrange("p (t m) -> p t m", t=PACK),
                        wa_raw[:].bitcast(U16).rearrange("p (m t) -> p t m", t=PACK))
 
-        page_words = sb.tile([P, I], U32, name="page_words", align_bytes=64)
+        nc.vector.tensor_copy(page_scales[:], pool_scales[:].indirect(idx[:]))
+        nc.vector.tensor_copy(wa_plane[:].rearrange("p (t m) -> p t m", t=PACK),
+                              wa_scales_raw[:].rearrange("p (m t) -> p t m", t=PACK))
+        page_words = sb.tile([P, I], U32, name="page_words", tag="wa_scales_raw", align_bytes=64)
         for h in range(2):
-            nc.vector.tensor_copy(page_scales[:, half(h)], pool_scales[:].indirect(idx[:, cols(h)]))
             nc.vector.tensor_copy(page_words[:, half(h)], pool_words[:].indirect(idx[:, cols(h)]))
-            planes = slice(0, 1) if h == 0 else slice(1, PACK)
-            nc.vector.tensor_copy(wa_plane[:].rearrange("p (t m) -> p t m", t=PACK)[:, planes, :],
-                                  wa_scales_raw[:].rearrange("p (m t) -> p t m", t=PACK)[:, planes, :])
 
         factor = sb.tile([P, PACK], F32, name="factor", tag="wa_raw", align_bytes=64)
         nc.sync.dma_start(factor[:], kf.rearrange("(p t) o -> p (t o)", t=PACK))
@@ -146,26 +145,26 @@ def tile_attend_pagerelay_kernel(tc, pages_words, pages_scales, wa_words, wa_sca
         looked = sb.tile([P, I], F32, name="looked")
         for h in range(2):
             nc.scalar.activation(looked[:, half(h)], f1[3][:].indirect(idx3[:, cols(h)]), COPY)
-        out_rows = out.rearrange("(j p) i -> p j i", p=P)
         for h in range(2):
             nc.vector.tensor_tensor(v[:, half(h)], looked[:, half(h)], z[3][:, half(h)], SUB)
+        for h in range(2):
             weigh(3, half(h), v)
-            codes = sb.tile([P, H], U32, name="codes_%d" % h, align_bytes=64)
-            plane = sb.tile([P, H], U8, name="plane_%d" % h, align_bytes=64)
-            nc.vector.quantize_mx(out=codes[:].bitcast(FP8X4), scales=plane[:],
+        codes = [sb.tile([P, H], U32, name="codes_%d" % h, align_bytes=64) for h in range(2)]
+        planes = [sb.tile([P, H], U8, name="plane_%d" % h, align_bytes=64) for h in range(2)]
+        for h in range(2):
+            nc.vector.quantize_mx(out=codes[h][:].bitcast(FP8X4), scales=planes[h][:],
                                   in_=w[:, half(h), :].rearrange("p i t -> p (i t)"))
+        out_rows = out.rearrange("(j p) i -> p j i", p=P)
+        for h in range(2):
             for j in range(2):
                 y = psum.tile([P, H], F32, name="bank_%d" % (2 * h + j))
                 nc.tensor.matmul_mx(out=y[:], lhsT=wo_codes[:, 2 * P * j:2 * P * (j + 1)].bitcast(FP4X4),
                                     lhsT_scale=wo_plane[:, P * j:P * (j + 1)],
-                                    rhs=codes[:].bitcast(FP8X4), rhs_scale=plane[:], start=True, stop=True)
+                                    rhs=codes[h][:].bitcast(FP8X4), rhs_scale=planes[h][:], start=True, stop=True)
                 res = sb.tile([P, H], F32, name="res_%d_%d" % (h, j))
-                if h == 1 and j == 0:
+                if j == 0:
                     nc.vector.tensor_copy(res[:], y[:])
                     nc.sync.dma_start(out_rows[:, j, half(h)], res[:])
-                elif h == 1:
-                    nc.scalar.copy(res[:], y[:])
-                    nc.scalar.dma_start(out_rows[:, j, half(h)], res[:])
                 else:
                     nc.scalar.copy(res[:], y[:])
-                    nc.sync.dma_start(out_rows[:, j, half(h)], res[:])
+                    nc.scalar.dma_start(out_rows[:, j, half(h)], res[:])

from contextlib import ExitStack

import concourse.mybir as mybir

D, K, T, M, I, E = 512, 512, 2048, 1024, 512, 256
FLOPS = 2 * D * K * I + 2 * K * E * I

F32 = mybir.dt.float32
BF16 = mybir.dt.bfloat16
I32 = mybir.dt.int32
U32 = mybir.dt.uint32
U16 = mybir.dt.uint16
U8 = mybir.dt.uint8
FP8X4 = mybir.dt.float8_e4m3fn_x4
FP4X4 = mybir.dt.float4_e2m1fn_x4
COPY = mybir.ActivationFunctionType.Copy
MULT = mybir.AluOpType.mult
SUB = mybir.AluOpType.subtract

P = 128
PACK = 4
H = I // 2
HC = H // 16
SHARE = 128


def tile_attend_pagerelay_kernel(tc, pages_words, pages_scales, wa_words, wa_scales, kf, wo_words, wo_scales,
                                  offs, offs2, offs3, out):
    nc = tc.nc
    with ExitStack() as ctx:
        lists = ctx.enter_context(tc.tile_pool(name="lists", bufs=1))
        sb = ctx.enter_context(tc.tile_pool(name="sb", bufs=1))
        psum = ctx.enter_context(tc.psum_pool(name="psum", bufs=1))

        def load_scale_rows(queue, plane, rows, q):
            queue.dma_start(plane[32 * q:32 * q + 4, :].bitcast(I32), rows[0, 4 * q:4 * q + 4, :].bitcast(I32))

        def half(h):
            return slice(h * H, (h + 1) * H)

        def cols(h):
            return slice(h * HC, (h + 1) * HC)

        idx = lists.tile([P, I // 16], U16, name="idx")
        idx2 = lists.tile([P, I // 16], U16, name="idx2")
        idx3 = lists.tile([P, I // 16], U16, name="idx3")
        pool_words = sb.tile([P, T], U32, name="pool_words", align_bytes=64)
        pool_scales = sb.tile([P, T], U8, name="pool_scales", align_bytes=64)
        wa_raw = sb.tile([P, 2 * K], U8, name="wa_raw", align_bytes=64)
        wa_scales_raw = sb.tile([P, K], U8, name="wa_scales_raw", align_bytes=64)
        wo_plane = sb.tile([P, E], U8, name="wo_plane", align_bytes=64)

        nc.vector.memset(pool_scales[:].bitcast(I32), 0)
        nc.vector.memset(wa_scales_raw[:].bitcast(I32), 0)

        staged = sb.tile([P, T], U8, name="staged", align_bytes=64)
        nc.sync.dma_start(idx[:], offs)
        for q in range(4):
            load_scale_rows(nc.sync if q < 2 else nc.scalar, staged, pages_scales, q)
        nc.scalar.dma_start(wa_raw[:].bitcast(I32), wa_words[0].bitcast(I32))
        nc.sync.dma_start(pool_words[:].bitcast(I32), pages_words[0].rearrange("p n t -> p (n t)").bitcast(I32))
        nc.sync.dma_start(idx2[:], offs2)
        nc.sync.dma_start(idx3[:], offs3)
        for q in range(4):
            load_scale_rows(nc.scalar, wa_scales_raw, wa_scales, q)
        f1 = [sb.tile([P, M], F32, name="f1_%d" % t) for t in range(PACK)]
        for t in range(PACK):
            (nc.vector if t % 2 else nc.gpsimd).memset(f1[t][:].bitcast(I32), 0)
        nc.gpsimd.memset(wo_plane[:].bitcast(I32), 0)

        for q in range(4):
            nc.vector.tensor_copy(pool_scales[32 * q:32 * q + 4, :].bitcast(I32), staged[32 * q:32 * q + 4, :].bitcast(I32))

        page_scales = sb.tile([P, I], U8, name="page_scales", align_bytes=64)

        wa_codes = sb.tile([P, 2 * K], U8, name="wa_codes", align_bytes=64)
        wa_plane = sb.tile([P, K], U8, name="wa_plane", align_bytes=64)
        nc.scalar.copy(wa_codes[:].bitcast(U16).rearrange("p (t m) -> p t m", t=PACK),
                       wa_raw[:].bitcast(U16).rearrange("p (m t) -> p t m", t=PACK))

        nc.vector.tensor_copy(page_scales[:], pool_scales[:].indirect(idx[:]))
        nc.vector.tensor_copy(wa_plane[:].rearrange("p (t m) -> p t m", t=PACK),
                              wa_scales_raw[:].rearrange("p (m t) -> p t m", t=PACK))
        page_words = sb.tile([P, I], U32, name="page_words", tag="wa_scales_raw", align_bytes=64)
        for h in range(2):
            nc.vector.tensor_copy(page_words[:, half(h)], pool_words[:].indirect(idx[:, cols(h)]))

        factor = sb.tile([P, PACK], F32, name="factor", tag="wa_raw", align_bytes=64)
        nc.sync.dma_start(factor[:], kf.rearrange("(p t) o -> p (t o)", t=PACK))
        wo_codes = sb.tile([P, 2 * E], U8, name="wo_codes", tag="staged", align_bytes=64)
        nc.sync.dma_start(wo_codes[:].bitcast(I32), wo_words[0].bitcast(I32))
        for q in range(4):
            load_scale_rows(nc.sync, wo_plane, wo_scales, q)

        def hidden(t, slots, bank):
            nc.tensor.matmul_mx(out=bank, lhsT=wa_codes[:, 2 * P * t:2 * P * (t + 1)].bitcast(FP4X4),
                                lhsT_scale=wa_plane[:, P * t:P * (t + 1)],
                                rhs=page_words[:, slots].bitcast(FP8X4), rhs_scale=page_scales[:, slots],
                                start=True, stop=True)

        z = [sb.tile([P, I], F32, name="z_%d" % t) for t in range(PACK)]
        every = slice(0, I)
        z0_banks = [psum.tile([P, H], F32, name="bank_%d" % h) for h in range(2)]
        for h in range(2):
            hidden(0, half(h), z0_banks[h][:])
        z1_bank = psum.tile([P, I], F32, name="bank_2")
        hidden(1, every, z1_bank[:])
        z3_first = psum.tile([P, SHARE], F32, name="bank_3")
        hidden(3, slice(0, SHARE), z3_first[:])
        z2_bank = psum.tile([P, I], F32, name="bank_4")
        hidden(2, every, z2_bank[:])
        z3_rest = psum.tile([P, I - SHARE], F32, name="bank_5")
        hidden(3, slice(SHARE, H), z3_rest[:, :H - SHARE])
        hidden(3, half(1), z3_rest[:, H - SHARE:])

        def put_scalar(t, slots):
            nc.scalar.activation(f1[t][:].indirect(idx2[:, slots.start // 16:slots.stop // 16]), z[t][:, slots], COPY)

        nc.vector.tensor_copy(z[1][:], z1_bank[:])
        nc.vector.tensor_copy(z[3][:, :SHARE], z3_first[:])
        nc.vector.tensor_copy(f1[1][:].indirect(idx2[:]), z[1][:])
        nc.vector.tensor_copy(f1[3][:].indirect(idx2[:, :SHARE // 16]), z[3][:, :SHARE])

        nc.scalar.copy(z[0][:, half(0)], z0_banks[0][:])
        put_scalar(0, half(0))
        nc.scalar.copy(z[0][:, half(1)], z0_banks[1][:])
        nc.scalar.copy(z[2][:], z2_bank[:])
        put_scalar(2, half(0))
        nc.scalar.copy(z[3][:, SHARE:], z3_rest[:])
        put_scalar(0, half(1))
        put_scalar(2, half(1))
        put_scalar(3, slice(SHARE, I))

        w = sb.tile([P, I, PACK], BF16, name="w", align_bytes=64)

        def weigh(t, slots, v):
            nc.vector.tensor_scalar(w[:, slots, t], v[:, slots], factor[:, t:t + 1], None, MULT)

        for n, t in enumerate((1, 0, 2)):
            v = sb.tile([P, I], F32, name="v_%d" % (n % 2))
            nc.vector.tensor_tensor(v[:], f1[t][:].indirect(idx3[:]), z[t][:], SUB)
            weigh(t, every, v)

        v = sb.tile([P, I], F32, name="v_0")
        looked = sb.tile([P, I], F32, name="looked")
        for h in range(2):
            nc.scalar.activation(looked[:, half(h)], f1[3][:].indirect(idx3[:, cols(h)]), COPY)
        for h in range(2):
            nc.vector.tensor_tensor(v[:, half(h)], looked[:, half(h)], z[3][:, half(h)], SUB)
        for h in range(2):
            weigh(3, half(h), v)
        codes = [sb.tile([P, H], U32, name="codes_%d" % h, align_bytes=64) for h in range(2)]
        planes = [sb.tile([P, H], U8, name="plane_%d" % h, align_bytes=64) for h in range(2)]
        for h in range(2):
            nc.vector.quantize_mx(out=codes[h][:].bitcast(FP8X4), scales=planes[h][:],
                                  in_=w[:, half(h), :].rearrange("p i t -> p (i t)"))
        out_rows = out.rearrange("(j p) i -> p j i", p=P)
        for h in range(2):
            for j in range(2):
                y = psum.tile([P, H], F32, name="bank_%d" % (2 * h + j))
                nc.tensor.matmul_mx(out=y[:], lhsT=wo_codes[:, 2 * P * j:2 * P * (j + 1)].bitcast(FP4X4),
                                    lhsT_scale=wo_plane[:, P * j:P * (j + 1)],
                                    rhs=codes[h][:].bitcast(FP8X4), rhs_scale=planes[h][:], start=True, stop=True)
                res = sb.tile([P, H], F32, name="res_%d_%d" % (h, j))
                if j == 0:
                    nc.vector.tensor_copy(res[:], y[:])
                    nc.sync.dma_start(out_rows[:, j, half(h)], res[:])
                else:
                    nc.scalar.copy(res[:], y[:])
                    nc.scalar.dma_start(out_rows[:, j, half(h)], res[:])
